import numpy as np
import ml_dtypes


def mxq(x, axis, fmt="e4m3"):
    dtype, down = {"e4m3": (ml_dtypes.float8_e4m3fn, 7), "e5m2": (ml_dtypes.float8_e5m2, 14)}[fmt]
    v = np.moveaxis(np.asarray(x, np.float32).astype(ml_dtypes.bfloat16).astype(np.float64), axis, -1)
    blocks = v.reshape(v.shape[:-1] + (-1, 32))
    amax = np.abs(blocks).max(-1, keepdims=True)
    byte = np.maximum(np.where(amax > 0, np.frexp(amax)[1] - 1 + 127, 0) - down, 1)
    scale = np.exp2(byte - 127.0)
    codes = (blocks / scale).astype(np.float32).astype(dtype).astype(np.float64)
    return np.moveaxis((codes * scale).reshape(v.shape), -1, axis)


WIDE = False


def mx_kscale(k):
    if not WIDE:
        return np.ones(k)
    levels = np.array([10, -10, 5, -5, 0])
    if k % 512:
        return np.exp2(np.random.permutation(np.resize(levels, k // 32))).repeat(32)
    a = np.empty((k // 512, 16))
    for p in range(k // 512):
        a[p, :8] = np.random.permutation(np.resize(levels, 8))
        for g in range(8):
            far = levels[np.abs(levels - a[p, g]) >= 10]
            a[p, g + 8] = far[np.random.randint(len(far))]
    return np.exp2(a.ravel()).repeat(32)


def f64(x):
    return np.asarray(x).astype(np.float64)


def striped(idx):
    return np.tile(idx.reshape(-1, 16).T, (8, 1)).astype(np.uint16)


def unstriped(offs):
    return offs[:16].T.reshape(-1).astype(np.int64)


E2M1 = np.array([0.0, 0.5, 1.0, 1.5, 2.0, 3.0, 4.0, 6.0, -0.0, -0.5, -1.0, -1.5, -2.0, -3.0, -4.0, -6.0])


def pack_weight(w, fmt):
    k, n = w.shape
    w = f64(np.asarray(w, np.float32).astype(ml_dtypes.bfloat16)).reshape(k // 32, 32, n)
    amax = np.abs(w).max(1)
    if fmt == "e4m3":
        byte = np.frexp(amax)[1] - 1 + 127 - 7
    else:
        mant, ex = np.frexp(amax / 6.0)
        byte = np.where(mant > 0.5, ex, ex - 1) + 127
    byte = np.clip(np.where(amax > 0, byte, 1), 1, 254)
    scaled = (w * np.exp2(127.0 - byte)[:, None, :]).reshape(k, n).astype(np.float32)
    by_word = np.ascontiguousarray(scaled.reshape(k // 512, 128, 4, n).transpose(0, 1, 3, 2))
    if fmt == "e4m3":
        words = by_word.astype(ml_dtypes.float8_e4m3fn).view(np.uint8)
    else:
        c = by_word.astype(ml_dtypes.float4_e2m1fn).view(np.uint8) & 0xF
        words = (c[..., 0::2] | (c[..., 1::2] << 4)).reshape(k // 512, 128, 2 * n)
    return np.ascontiguousarray(words), np.ascontiguousarray(byte.astype(np.uint8).reshape(k // 512, 16, n))


def unpack_weight(words, scales, fmt):
    g, _, n = scales.shape
    words = np.ascontiguousarray(words).reshape(g, 128, n, -1)
    if fmt == "e4m3":
        vals = words.view(ml_dtypes.float8_e4m3fn).astype(np.float64)
    else:
        nib = np.empty((g, 128, n, 4), np.uint8)
        nib[..., 0::2] = words & 0xF
        nib[..., 1::2] = words >> 4
        vals = E2M1[nib]
    vals = vals * np.repeat(np.exp2(scales.astype(np.float64) - 127.0), 8, axis=1)[..., None]
    return vals.transpose(0, 1, 3, 2).reshape(g * 512, n)


def gelu(v):
    return 0.5 * v * (1.0 + np.tanh(np.sqrt(2.0 / np.pi) * (v + 0.044715 * v**3)))


K, H, N, T, S, T2, P = 512, 1024, 512, 2048, 1024, 2048, 1024

def setup_inputs():
    n = np.random.standard_normal
    s = mx_kscale(K)[:, None]
    u = mx_kscale(H)[:, None]
    tab_words, tab_scales = pack_weight(n((K, T)) * s, "e4m3")
    w4_words, w4_scales = pack_weight(n((K, H)) / np.sqrt(K) / s * u.T, "e2m1")
    ro8_words, ro8_scales = pack_weight(n((H, N)) / np.sqrt(H) / u, "e4m3")
    return {
        "tab_words": tab_words, "tab_scales": tab_scales,
        "offs": striped(np.random.permutation(T)[:S]),
        "w4_words": w4_words, "w4_scales": w4_scales,
        "page0": (n((H, T2)) * u).astype(np.float32),
        "wgs": np.exp(0.3 * n((128, S))).astype(np.float32),
        "offs2": striped(np.random.permutation(T2)[:S]),
        "offs3": striped(np.random.permutation(T2)[:P]),
        "stim": (0.8 * n((H, P)) * u).astype(np.float32),
        "cpl": (n((H, N)) / np.sqrt(H) / u).astype(np.float32),
        "ro8_words": ro8_words, "ro8_scales": ro8_scales,
    }

def reference(tab_words, tab_scales, offs, w4_words, w4_scales, page0, wgs, offs2, offs3,
              stim, cpl, ro8_words, ro8_scales):
    v = unpack_weight(tab_words, tab_scales, "e4m3")[:, unstriped(offs)]
    h = unpack_weight(w4_words, w4_scales, "e2m1").T @ v
    page = f64(page0).copy()
    page[:, unstriped(offs2)] = np.tile(f64(wgs), (H // 128, 1)) * h
    x = page[:, unstriped(offs3)]
    z = x + f64(stim)
    xq = mxq(x, 0, "e4m3")
    zq = mxq(z, 0, "e4m3")
    cq = mxq(f64(cpl), 0, "e4m3")
    y = unpack_weight(ro8_words, ro8_scales, "e4m3").T @ zq
    y = y + np.tanh(cq.T @ xq)
    y = y + np.tanh(cq.T @ zq)
    return y

@@ -1,0 +1,210 @@
+from contextlib import ExitStack
+
+import concourse.mybir as mybir
+
+K, H, N, T, S, T2, M = 512, 1024, 512, 2048, 1024, 2048, 1024
+FLOPS = 2 * K * H * S + 3 * 2 * H * N * M
+
+F32 = mybir.dt.float32
+BF16 = mybir.dt.bfloat16
+I32 = mybir.dt.int32
+U32 = mybir.dt.uint32
+U16 = mybir.dt.uint16
+U8 = mybir.dt.uint8
+FP8X4 = mybir.dt.float8_e4m3fn_x4
+FP4X4 = mybir.dt.float4_e2m1fn_x4
+MULT = mybir.AluOpType.mult
+ADD = mybir.AluOpType.add
+TANH = mybir.ActivationFunctionType.Tanh
+
+P = 128
+PACK = 4
+K_PASS = P * PACK
+PASSES = H // K_PASS
+BANK = 512
+CHUNK = 256
+CHUNKS = M // CHUNK
+LIST_ROWS = 16
+
+
+def tile_list_parcel_coupling_readout_kernel(
+    tc, tab_words, tab_scales, offs, w4_words, w4_scales, page0, wgs, offs2, offs3,
+    stim, cpl, ro8_words, ro8_scales, out,
+):
+    nc = tc.nc
+    with ExitStack() as ctx:
+        keep = ctx.enter_context(tc.tile_pool(name="keep", bufs=1))
+        pages = ctx.enter_context(tc.tile_pool(name="pages", bufs=4))
+        ring = ctx.enter_context(tc.tile_pool(name="ring", bufs=3))
+        psum = ctx.enter_context(tc.psum_pool(name="psum", bufs=2))
+
+        def list_slice(tile, first, count):
+            return tile[:, first // LIST_ROWS : (first + count) // LIST_ROWS]
+
+        def load_scale_rows(queue, plane, rows, per_quadrant):
+            for q in range(4):
+                queue.dma_start(
+                    out=plane[32 * q : 32 * q + per_quadrant, :].bitcast(I32),
+                    in_=rows(q).bitcast(I32),
+                )
+
+        tab_s = keep.tile([P, T], U8, align_bytes=64)
+        w4_s_raw = keep.tile([P, H], U8, align_bytes=64)
+        ro_s = keep.tile([P, N], U8, align_bytes=64)
+        nc.vector.memset(tab_s[:].bitcast(I32), 0)
+        nc.gpsimd.memset(w4_s_raw[:].bitcast(I32), 0)
+        load_scale_rows(nc.gpsimd, w4_s_raw, lambda q: w4_scales[0, 4 * q : 4 * q + 4, :], 4)
+
+        idx = keep.tile([P, S // LIST_ROWS], U16)
+        nc.sync.dma_start(idx[:], offs)
+        load_scale_rows(nc.sync, tab_s, lambda q: tab_scales[0, 4 * q : 4 * q + 4, :], 4)
+        idx2 = keep.tile([P, S // LIST_ROWS], U16)
+        nc.sync.dma_start(idx2[:], offs2)
+        idx3 = keep.tile([P, M // LIST_ROWS], U16)
+        nc.sync.dma_start(idx3[:], offs3)
+        w4_w_raw = keep.tile([P, H], U16, align_bytes=64)
+        nc.sync.dma_start(out=w4_w_raw[:].bitcast(I32), in_=w4_words[0].bitcast(I32))
+        tab_w = keep.tile([P, T], U32, align_bytes=64)
+        nc.sync.dma_start(out=tab_w[:].bitcast(I32), in_=tab_words[0].rearrange("p t i -> p (t i)").bitcast(I32))
+
+        def load_page(a, t):
+            page = pages.tile([P, T2], F32, name="page")
+            rows = page0[a * K_PASS : (a + 1) * K_PASS, :].rearrange("(p t) c -> t p c", t=PACK)
+            nc.sync.dma_start(out=page[:], in_=rows[t])
+            return page
+
+        def load_gains(first, last):
+            gain = keep.tile([P, last - first, S], F32, name="gain%d" % first)
+            rows = wgs.rearrange("(q t) j -> q t j", t=PACK)[:, first:last, :]
+            for q in range(4):
+                nc.sync.dma_start(out=gain[32 * q : 32 * q + 32, :, :], in_=rows)
+            return [gain[:, t, :] for t in range(last - first)]
+
+        gains = load_gains(0, 1)
+        page_tiles = {(0, 0): load_page(0, 0), (0, 1): load_page(0, 1)}
+        gains.extend(load_gains(1, PACK))
+
+        w4_w = keep.tile([P, H], U16, align_bytes=64)
+        w4_s = keep.tile([P, H], U8, align_bytes=64)
+        for dst, src in ((w4_w, w4_w_raw), (w4_s, w4_s_raw)):
+            nc.vector.tensor_copy(
+                out=dst[:].rearrange("p (a t m) -> p a t m", a=PASSES, t=PACK),
+                in_=src[:].rearrange("p (a m t) -> p a t m", a=PASSES, t=PACK),
+            )
+
+        v_w = [keep.tile([P, BANK], U32, align_bytes=64, name="v_w%d" % u) for u in range(S // BANK)]
+        v_s = [keep.tile([P, BANK], U8, align_bytes=64, name="v_s%d" % u) for u in range(S // BANK)]
+        for u in range(S // BANK):
+            nc.vector.tensor_copy(v_s[u][:], tab_s[:].indirect(list_slice(idx, u * BANK, BANK)))
+            nc.vector.tensor_copy(v_w[u][:], tab_w[:].indirect(list_slice(idx, u * BANK, BANK)))
+
+        def reset_rows(a, t):
+            cols = slice((a * PACK + t) * P, (a * PACK + t + 1) * P)
+            h = ring.tile([P, S], F32, name="plane")
+            for u in range(S // BANK):
+                h_bank = psum.tile([P, BANK], F32, name="h_bank")
+                nc.tensor.matmul_mx(
+                    out=h_bank[:],
+                    lhsT=w4_w[:, cols].bitcast(U8).bitcast(FP4X4), lhsT_scale=w4_s[:, cols],
+                    rhs=v_w[u][:].bitcast(FP8X4), rhs_scale=v_s[u][:],
+                    start=True, stop=True,
+                )
+                nc.scalar.copy(out=h[:, u * BANK : (u + 1) * BANK], in_=h_bank[:])
+            nc.vector.tensor_tensor(page_tiles[a, t][:].indirect(idx2[:]), h[:], gains[t], MULT)
+
+        def load_stim(a):
+            rows = keep.tile([P, PACK, M], F32, name="stim_rows")
+            nc.sync.dma_start(out=rows[:], in_=stim[a * K_PASS : (a + 1) * K_PASS, :].rearrange("(p t) m -> p t m", t=PACK))
+            return rows
+
+        def walk_planes(planes):
+            return planes.rearrange("p t (c i) -> p c t i", i=PACK)
+
+        def walk_grouped(grouped):
+            return grouped.rearrange("p (c i t) -> p c t i", i=PACK, t=PACK)
+
+        def quantise_chunk(a, c, x_planes, stim_planes):
+            grouped = ring.tile([P, 2 * CHUNK * PACK], BF16, align_bytes=64, name="grouped")
+            nc.scalar.copy(out=walk_grouped(grouped[:, : CHUNK * PACK]), in_=walk_planes(x_planes))
+            nc.vector.tensor_tensor(walk_grouped(grouped[:, CHUNK * PACK :]), walk_planes(x_planes), walk_planes(stim_planes), ADD)
+            codes = keep.tile([P, 2 * CHUNK], U32, align_bytes=64, name="xz_w%d_%d" % (a, c))
+            scales = keep.tile([P, 2 * CHUNK], U8, align_bytes=64, name="xz_s%d_%d" % (a, c))
+            nc.vector.quantize_mx(out=codes[:].bitcast(FP8X4), scales=scales[:], in_=grouped[:])
+            return codes, scales
+
+        x0 = keep.tile([P, PACK, M], F32)
+        for t in range(PACK):
+            if t + 2 < PACK:
+                page_tiles[0, t + 2] = load_page(0, t + 2)
+            reset_rows(0, t)
+            nc.vector.tensor_copy(x0[:, t, :], page_tiles[0, t][:].indirect(idx3[:]))
+        stim0 = load_stim(0)
+
+        cpl_w, cpl_s = [], []
+        for a in range(PASSES):
+            raw = keep.tile([P, PACK, N], F32, name="cpl_raw%d" % a)
+            nc.sync.dma_start(out=raw[:], in_=cpl[a * K_PASS : (a + 1) * K_PASS, :].rearrange("(p t) n -> p t n", t=PACK))
+            grouped = ring.tile([P, N * PACK], BF16, align_bytes=64, name="grouped")
+            nc.scalar.copy(out=walk_grouped(grouped[:]), in_=walk_planes(raw[:]))
+            codes = keep.tile([P, N], U32, align_bytes=64, name="cpl_w%d" % a)
+            scales = keep.tile([P, N], U8, align_bytes=64, name="cpl_s%d" % a)
+            nc.vector.quantize_mx(out=codes[:].bitcast(FP8X4), scales=scales[:], in_=grouped[:])
+            cpl_w.append(codes)
+            cpl_s.append(scales)
+
+        ro_w = keep.tile([P, PASSES, N], U32, align_bytes=64)
+        nc.sync.dma_start(out=ro_w[:].bitcast(I32), in_=ro8_words.rearrange("a p c i -> p a (c i)").bitcast(I32))
+        nc.vector.memset(ro_s[:].bitcast(I32), 0)
+        load_scale_rows(nc.sync, ro_s, lambda q: ro8_scales[:, 4 * q : 4 * q + 4, :], 8)
+
+        xz = {}
+        for t in range(PACK):
+            page_tiles[1, t] = load_page(1, t)
+            reset_rows(1, t)
+            cols = slice(t * CHUNK, (t + 1) * CHUNK)
+            xz[0, t] = quantise_chunk(0, t, x0[:, :, cols], stim0[:, :, cols])
+        stim1 = load_stim(1)
+
+        def fetch_chunk(c):
+            x1 = ring.tile([P, PACK, CHUNK], F32, name="plane")
+            for t in range(PACK):
+                nc.vector.tensor_copy(x1[:, t, :], page_tiles[1, t][:].indirect(list_slice(idx3, c * CHUNK, CHUNK)))
+            xz[1, c] = quantise_chunk(1, c, x1[:], stim1[:, :, c * CHUNK : (c + 1) * CHUNK])
+
+        def read_out(c, pair):
+            y_bank = psum.tile([P, 2, CHUNK], F32, name="y_bank")
+            ab_banks = [psum.tile([P, 2, CHUNK], F32, name="ab_bank%d" % b) for b in range(2)]
+            for a in range(PASSES):
+                codes, scales = xz[a, c]
+                for b in range(2):
+                    cols = slice((2 * pair + b) * P, (2 * pair + b + 1) * P)
+                    nc.tensor.matmul_mx(
+                        out=ab_banks[b][:].rearrange("p s m -> p (s m)"),
+                        lhsT=cpl_w[a][:, cols].bitcast(FP8X4), lhsT_scale=cpl_s[a][:, cols],
+                        rhs=codes[:].bitcast(FP8X4), rhs_scale=scales[:],
+                        start=(a == 0), stop=(a == PASSES - 1),
+                    )
+                for b in range(2):
+                    cols = slice((2 * pair + b) * P, (2 * pair + b + 1) * P)
+                    nc.tensor.matmul_mx(
+                        out=y_bank[:, b, :],
+                        lhsT=ro_w[:, a, cols].bitcast(FP8X4), lhsT_scale=ro_s[4 * a :, cols],
+                        rhs=codes[:, CHUNK:].bitcast(FP8X4), rhs_scale=scales[:, CHUNK:],
+                        start=(a == 0 and b == 0), stop=(a == PASSES - 1 and b == 1),
+                    )
+            bent = ring.tile([P, 2, 2, CHUNK], F32, name="bent")
+            for b in range(2):
+                nc.scalar.activation(bent[:, b, :, :], ab_banks[b][:], TANH)
+            partial = ring.tile([P, 2, CHUNK], F32, name="partial")
+            nc.vector.tensor_tensor(partial[:], y_bank[:], bent[:, :, 0, :], ADD)
+            result = ring.tile([P, 2, CHUNK], F32, name="result")
+            nc.vector.tensor_tensor(result[:], partial[:], bent[:, :, 1, :], ADD)
+            rows = out[2 * pair * P : (2 * pair + 2) * P, c * CHUNK : (c + 1) * CHUNK]
+            nc.sync.dma_start(out=rows.rearrange("(b p) m -> p b m", p=P), in_=result[:])
+
+        fetch_chunk(0)
+        for c in range(CHUNKS):
+            if c + 1 < CHUNKS:
+                fetch_chunk(c + 1)
+            for pair in range(2):
+                read_out(c, pair)

@@ -1,6 +1,7 @@
 from contextlib import ExitStack
 
 import concourse.mybir as mybir
+from concourse.masks import make_identity
 
 K, H, N, T, S, T2, M = 512, 1024, 512, 2048, 1024, 2048, 1024
 FLOPS = 2 * K * H * S + 3 * 2 * H * N * M
@@ -18,13 +19,25 @@ ADD = mybir.AluOpType.add
 TANH = mybir.ActivationFunctionType.Tanh
 
 P = 128
+QUADRANT = 32
 PACK = 4
 K_PASS = P * PACK
 PASSES = H // K_PASS
 BANK = 512
 CHUNK = 256
 CHUNKS = M // CHUNK
+BLOCKS = CHUNK // P
 LIST_ROWS = 16
+PAIR = 2
+PAGE_BUFS = 4
+RING_BUFS = 3
+GROUPED_BUFS = CHUNKS
+
+COUPLING_BANKS = (0, 1, 2, 3, 4)
+READOUT_BANKS = (5, 6, 7)
+H_BANKS = (0, 1, 2)
+TURN_BANKS = (3, 4)
+BACK_BANK = 7
 
 
 def tile_list_parcel_coupling_readout_kernel(
@@ -34,177 +47,261 @@ def tile_list_parcel_coupling_readout_kernel(
     nc = tc.nc
     with ExitStack() as ctx:
         keep = ctx.enter_context(tc.tile_pool(name="keep", bufs=1))
-        pages = ctx.enter_context(tc.tile_pool(name="pages", bufs=4))
-        ring = ctx.enter_context(tc.tile_pool(name="ring", bufs=3))
-        psum = ctx.enter_context(tc.psum_pool(name="psum", bufs=2))
+        pages = ctx.enter_context(tc.tile_pool(name="pages", bufs=PAGE_BUFS))
+        ring = ctx.enter_context(tc.tile_pool(name="ring", bufs=RING_BUFS))
+        psum = ctx.enter_context(tc.psum_pool(name="psum", bufs=1))
 
-        def list_slice(tile, first, count):
+        def held(name, shape, dtype, tag=None):
+            return keep.tile(shape, dtype, align_bytes=64, name=name, tag=tag or name)
+
+        def bank(banks, turn, shape):
+            return psum.tile(shape, F32, name="bank%d" % banks[turn % len(banks)])
+
+        def load_list(name, source):
+            tile = held(name, list(source.shape), U16)
+            nc.sync.dma_start(tile[:], source)
+            return tile
+
+        def entries(tile, first, count):
             return tile[:, first // LIST_ROWS : (first + count) // LIST_ROWS]
 
-        def load_scale_rows(queue, plane, rows, per_quadrant):
-            for q in range(4):
-                queue.dma_start(
-                    out=plane[32 * q : 32 * q + per_quadrant, :].bitcast(I32),
-                    in_=rows(q).bitcast(I32),
+        def load_scales(tile, source):
+            rows = PACK * source.shape[0]
+            for q in range(P // QUADRANT):
+                nc.sync.dma_start(
+                    out=tile[QUADRANT * q : QUADRANT * q + rows, :].bitcast(I32),
+                    in_=source[:, PACK * q : PACK * (q + 1), :].bitcast(I32),
                 )
 
-        tab_s = keep.tile([P, T], U8, align_bytes=64)
-        w4_s_raw = keep.tile([P, H], U8, align_bytes=64)
-        ro_s = keep.tile([P, N], U8, align_bytes=64)
-        nc.vector.memset(tab_s[:].bitcast(I32), 0)
-        nc.gpsimd.memset(w4_s_raw[:].bitcast(I32), 0)
-        load_scale_rows(nc.gpsimd, w4_s_raw, lambda q: w4_scales[0, 4 * q : 4 * q + 4, :], 4)
+        def pass_rows(source, a):
+            return source[a * K_PASS : (a + 1) * K_PASS, :].rearrange("(p t) c -> p t c", t=PACK)
 
-        idx = keep.tile([P, S // LIST_ROWS], U16)
-        nc.sync.dma_start(idx[:], offs)
-        load_scale_rows(nc.sync, tab_s, lambda q: tab_scales[0, 4 * q : 4 * q + 4, :], 4)
-        idx2 = keep.tile([P, S // LIST_ROWS], U16)
-        nc.sync.dma_start(idx2[:], offs2)
-        idx3 = keep.tile([P, M // LIST_ROWS], U16)
-        nc.sync.dma_start(idx3[:], offs3)
-        w4_w_raw = keep.tile([P, H], U16, align_bytes=64)
-        nc.sync.dma_start(out=w4_w_raw[:].bitcast(I32), in_=w4_words[0].bitcast(I32))
-        tab_w = keep.tile([P, T], U32, align_bytes=64)
-        nc.sync.dma_start(out=tab_w[:].bitcast(I32), in_=tab_words[0].rearrange("p t i -> p (t i)").bitcast(I32))
+        def load_planes(name, source, a, first=0, count=PACK, tag=None):
+            tile = held(name, [P, count, source.shape[1]], F32, tag)
+            nc.sync.dma_start(out=tile[:], in_=pass_rows(source, a)[:, first : first + count, :])
+            return tile
 
         def load_page(a, t):
             page = pages.tile([P, T2], F32, name="page")
-            rows = page0[a * K_PASS : (a + 1) * K_PASS, :].rearrange("(p t) c -> t p c", t=PACK)
-            nc.sync.dma_start(out=page[:], in_=rows[t])
+            nc.sync.dma_start(out=page[:], in_=pass_rows(page0, a)[:, t, :])
             return page
 
-        def load_gains(first, last):
-            gain = keep.tile([P, last - first, S], F32, name="gain%d" % first)
-            rows = wgs.rearrange("(q t) j -> q t j", t=PACK)[:, first:last, :]
-            for q in range(4):
-                nc.sync.dma_start(out=gain[32 * q : 32 * q + 32, :, :], in_=rows)
-            return [gain[:, t, :] for t in range(last - first)]
+        def load_gain(t):
+            gain = held("gain%d" % t, [P, S], F32)
+            rows = wgs.rearrange("(q t) j -> q t j", t=PACK)[:, t, :]
+            for q in range(P // QUADRANT):
+                nc.sync.dma_start(out=gain[QUADRANT * q : QUADRANT * (q + 1), :], in_=rows)
+            return gain
 
-        gains = load_gains(0, 1)
-        page_tiles = {(0, 0): load_page(0, 0), (0, 1): load_page(0, 1)}
-        gains.extend(load_gains(1, PACK))
+        def chunk_cols(c):
+            return slice(c * CHUNK, (c + 1) * CHUNK)
 
-        w4_w = keep.tile([P, H], U16, align_bytes=64)
-        w4_s = keep.tile([P, H], U8, align_bytes=64)
-        for dst, src in ((w4_w, w4_w_raw), (w4_s, w4_s_raw)):
-            nc.vector.tensor_copy(
-                out=dst[:].rearrange("p (a t m) -> p a t m", a=PASSES, t=PACK),
-                in_=src[:].rearrange("p (a m t) -> p a t m", a=PASSES, t=PACK),
+        def interleave(grouped, first, planes):
+            places = grouped.rearrange("p (c i t) -> p c t i", i=PACK, t=PACK)
+            nc.scalar.copy(
+                out=places[:, :, first : first + planes.shape[1], :],
+                in_=planes.rearrange("p t (c i) -> p c t i", i=PACK),
             )
 
-        v_w = [keep.tile([P, BANK], U32, align_bytes=64, name="v_w%d" % u) for u in range(S // BANK)]
-        v_s = [keep.tile([P, BANK], U8, align_bytes=64, name="v_s%d" % u) for u in range(S // BANK)]
-        for u in range(S // BANK):
-            nc.vector.tensor_copy(v_s[u][:], tab_s[:].indirect(list_slice(idx, u * BANK, BANK)))
-            nc.vector.tensor_copy(v_w[u][:], tab_w[:].indirect(list_slice(idx, u * BANK, BANK)))
-
-        def reset_rows(a, t):
-            cols = slice((a * PACK + t) * P, (a * PACK + t + 1) * P)
-            h = ring.tile([P, S], F32, name="plane")
-            for u in range(S // BANK):
-                h_bank = psum.tile([P, BANK], F32, name="h_bank")
-                nc.tensor.matmul_mx(
-                    out=h_bank[:],
-                    lhsT=w4_w[:, cols].bitcast(U8).bitcast(FP4X4), lhsT_scale=w4_s[:, cols],
-                    rhs=v_w[u][:].bitcast(FP8X4), rhs_scale=v_s[u][:],
-                    start=True, stop=True,
-                )
-                nc.scalar.copy(out=h[:, u * BANK : (u + 1) * BANK], in_=h_bank[:])
-            nc.vector.tensor_tensor(page_tiles[a, t][:].indirect(idx2[:]), h[:], gains[t], MULT)
-
-        def load_stim(a):
-            rows = keep.tile([P, PACK, M], F32, name="stim_rows")
-            nc.sync.dma_start(out=rows[:], in_=stim[a * K_PASS : (a + 1) * K_PASS, :].rearrange("(p t) m -> p t m", t=PACK))
-            return rows
-
-        def walk_planes(planes):
-            return planes.rearrange("p t (c i) -> p c t i", i=PACK)
-
-        def walk_grouped(grouped):
-            return grouped.rearrange("p (c i t) -> p c t i", i=PACK, t=PACK)
-
-        def quantise_chunk(a, c, x_planes, stim_planes):
-            grouped = ring.tile([P, 2 * CHUNK * PACK], BF16, align_bytes=64, name="grouped")
-            nc.scalar.copy(out=walk_grouped(grouped[:, : CHUNK * PACK]), in_=walk_planes(x_planes))
-            nc.vector.tensor_tensor(walk_grouped(grouped[:, CHUNK * PACK :]), walk_planes(x_planes), walk_planes(stim_planes), ADD)
-            codes = keep.tile([P, 2 * CHUNK], U32, align_bytes=64, name="xz_w%d_%d" % (a, c))
-            scales = keep.tile([P, 2 * CHUNK], U8, align_bytes=64, name="xz_s%d_%d" % (a, c))
+        def quantise(name, grouped, tag=None):
+            width = grouped.shape[1] // PACK
+            codes = held(name + "_codes", [P, width], U32, tag)
+            scales = held(name + "_scales", [P, width], U8)
             nc.vector.quantize_mx(out=codes[:].bitcast(FP8X4), scales=scales[:], in_=grouped[:])
             return codes, scales
 
-        x0 = keep.tile([P, PACK, M], F32)
+        tab_s = held("tab_s", [P, T], U8)
+        w4_s_raw = held("w4_s_raw", [P, H], U8)
+        nc.gpsimd.memset(tab_s[:].bitcast(I32), 0)
+        nc.vector.memset(w4_s_raw[:].bitcast(I32), 0)
+        w4_w_raw = held("w4_w_raw", [P, H], U16)
+        nc.sync.dma_start(out=w4_w_raw[:].bitcast(I32), in_=w4_words[0].bitcast(I32))
+        idx = load_list("idx", offs)
+        load_scales(tab_s, tab_scales)
+        tab_w = held("tab_w", [P, T], U32)
+        nc.sync.dma_start(out=tab_w[:].bitcast(I32), in_=tab_words[0].rearrange("p t i -> p (t i)").bitcast(I32))
+        load_scales(w4_s_raw, w4_scales)
+        ident = held("ident", [P, P], F32)
+        make_identity(nc, ident[:])
+        page_tiles = {(0, 0): load_page(0, 0)}
+        idx2 = load_list("idx2", offs2)
+        gains = [load_gain(0)]
+        page_tiles[0, 1] = load_page(0, 1)
+        idx3 = load_list("idx3", offs3)
+        gains.append(load_gain(1))
+
+        def columns_by_plane(name, raw):
+            tile = held(name, [P, H], raw.dtype)
+            nc.vector.tensor_copy(
+                out=tile[:].rearrange("p (a t m) -> p a t m", a=PASSES, t=PACK),
+                in_=raw[:].rearrange("p (a m t) -> p a t m", a=PASSES, t=PACK),
+            )
+            return tile
+
+        def gather_table(name, table, half, tag=None):
+            tile = held("%s%d" % (name, half), [P, BANK], table.dtype, tag)
+            nc.vector.tensor_copy(tile[:], table[:].indirect(entries(idx, half * BANK, BANK)))
+            return tile
+
+        w4_w = columns_by_plane("w4_w", w4_w_raw)
+        v_s = [gather_table("v_s", tab_s, 0)]
+        v_w = [gather_table("v_w", tab_w, 0)]
+        w4_s = columns_by_plane("w4_s", w4_s_raw)
+        v_s.append(gather_table("v_s", tab_s, 1))
+        v_w.append(gather_table("v_w", tab_w, 1, tag="w4_s_raw"))
+
+        def reset_plane(a, t):
+            plane = a * PACK + t
+            cols = slice(plane * P, (plane + 1) * P)
+            h = held("h%d_%d" % (a, t), [P, S], F32)
+            for half in range(S // BANK):
+                h_bank = bank(H_BANKS, plane * (S // BANK) + half, [P, BANK])
+                nc.tensor.matmul_mx(
+                    out=h_bank[:],
+                    lhsT=w4_w[:, cols].bitcast(U8).bitcast(FP4X4), lhsT_scale=w4_s[:, cols],
+                    rhs=v_w[half][:].bitcast(FP8X4), rhs_scale=v_s[half][:],
+                    start=True, stop=True,
+                )
+                nc.scalar.copy(out=h[:, half * BANK : (half + 1) * BANK], in_=h_bank[:])
+            width = BANK if plane == 0 else S
+            for first in range(0, S, width):
+                js = slice(first, first + width)
+                window = page_tiles[a, t][:].indirect(entries(idx2, first, width))
+                nc.vector.tensor_tensor(window, h[:, js], gains[t][:, js], MULT)
+
+        def fetch(dst, a, t, first, count):
+            nc.vector.tensor_copy(dst, page_tiles[a, t][:].indirect(entries(idx3, first, count)))
+
+        def add_by_transposes(c, z_words, x_planes, stim_planes):
+            words = x_planes.shape[1] // PAIR
+            pieces = [(b, u) for b in range(BLOCKS) for u in range(words)]
+            per_bank = BANK // (PAIR * P)
+            back = bank((BACK_BANK,), 0, [P, BLOCKS, words, P])
+            for turn in range(len(pieces) // per_bank):
+                mine = pieces[turn * per_bank : (turn + 1) * per_bank]
+                sums = bank(TURN_BANKS, c + turn, [P, per_bank, PAIR, P])
+                terms = [(planes, i, e) for planes in (stim_planes, x_planes) for i in range(per_bank) for e in range(PAIR)]
+                for number, (planes, i, e) in enumerate(terms):
+                    b, u = mine[i]
+                    nc.tensor.matmul(
+                        sums[:, i, e, :], planes[:, PAIR * u + e, b * P : (b + 1) * P], ident[:], is_transpose=True,
+                        start=(number == 0), stop=(number == len(terms) - 1),
+                    )
+                turned = ring.tile([P, per_bank, P, PAIR], BF16, name="turned")
+                nc.scalar.copy(out=turned[:], in_=sums[:].rearrange("m i e p -> m i p e"))
+                turned_words = turned[:].rearrange("m i p e -> m i (p e)").bitcast(F32)
+                for i, (b, u) in enumerate(mine):
+                    nc.tensor.transpose(back[:, b, u, :], turned_words[:, i, :], ident[:])
+            nc.scalar.copy(out=z_words.rearrange("p (b m) u -> p b m u", b=BLOCKS), in_=back[:].rearrange("p b u m -> p b m u"))
+
+        def column_words(grouped):
+            return grouped.bitcast(F32).rearrange("p (m u) -> p m u", u=PACK // PAIR)
+
+        x_part, z_part = slice(0, CHUNK * PACK), slice(CHUNK * PACK, 2 * CHUNK * PACK)
+
+        coupling = []
+        for a in range(PASSES):
+            cpl_planes = load_planes("cpl_planes%d" % a, cpl, a)
+            grouped = ring.tile([P, N * PACK], BF16, align_bytes=64, name="grouped", bufs=GROUPED_BUFS)
+            interleave(grouped[:], 0, cpl_planes[:])
+            coupling.append(quantise("cpl%d" % a, grouped))
+
+        x_first = held("x_first", [P, PACK, M], F32)
         for t in range(PACK):
             if t + 2 < PACK:
                 page_tiles[0, t + 2] = load_page(0, t + 2)
-            reset_rows(0, t)
-            nc.vector.tensor_copy(x0[:, t, :], page_tiles[0, t][:].indirect(idx3[:]))
-        stim0 = load_stim(0)
+                gains.append(load_gain(t + 2))
+            reset_plane(0, t)
+            fetch(x_first[:, t, :], 0, t, 0, M)
+        stim_first = load_planes("stim_first", stim, 0)
 
-        cpl_w, cpl_s = [], []
-        for a in range(PASSES):
-            raw = keep.tile([P, PACK, N], F32, name="cpl_raw%d" % a)
-            nc.sync.dma_start(out=raw[:], in_=cpl[a * K_PASS : (a + 1) * K_PASS, :].rearrange("(p t) n -> p t n", t=PACK))
-            grouped = ring.tile([P, N * PACK], BF16, align_bytes=64, name="grouped")
-            nc.scalar.copy(out=walk_grouped(grouped[:]), in_=walk_planes(raw[:]))
-            codes = keep.tile([P, N], U32, align_bytes=64, name="cpl_w%d" % a)
-            scales = keep.tile([P, N], U8, align_bytes=64, name="cpl_s%d" % a)
-            nc.vector.quantize_mx(out=codes[:].bitcast(FP8X4), scales=scales[:], in_=grouped[:])
-            cpl_w.append(codes)
-            cpl_s.append(scales)
-
-        ro_w = keep.tile([P, PASSES, N], U32, align_bytes=64)
+        ro_w = held("ro_w", [P, PASSES, N], U32)
         nc.sync.dma_start(out=ro_w[:].bitcast(I32), in_=ro8_words.rearrange("a p c i -> p a (c i)").bitcast(I32))
+        ro_s = held("ro_s", [P, N], U8)
         nc.vector.memset(ro_s[:].bitcast(I32), 0)
-        load_scale_rows(nc.sync, ro_s, lambda q: ro8_scales[:, 4 * q : 4 * q + 4, :], 8)
+        load_scales(ro_s, ro8_scales)
 
-        xz = {}
+        x_early = held("x_early", [P, PAIR, M], F32)
+        first_grouped = []
         for t in range(PACK):
             page_tiles[1, t] = load_page(1, t)
-            reset_rows(1, t)
-            cols = slice(t * CHUNK, (t + 1) * CHUNK)
-            xz[0, t] = quantise_chunk(0, t, x0[:, :, cols], stim0[:, :, cols])
-        stim1 = load_stim(1)
+            reset_plane(1, t)
+            if t < PAIR:
+                fetch(x_early[:, t, :], 1, t, 0, M)
+            grouped = ring.tile([P, 2 * CHUNK * PACK], BF16, align_bytes=64, name="grouped", bufs=GROUPED_BUFS)
+            add_by_transposes(t, column_words(grouped[:, z_part]), x_first[:, :, chunk_cols(t)], stim_first[:, :, chunk_cols(t)])
+            interleave(grouped[:, x_part], 0, x_first[:, :, chunk_cols(t)])
+            first_grouped.append(grouped)
 
-        def fetch_chunk(c):
-            x1 = ring.tile([P, PACK, CHUNK], F32, name="plane")
-            for t in range(PACK):
-                nc.vector.tensor_copy(x1[:, t, :], page_tiles[1, t][:].indirect(list_slice(idx3, c * CHUNK, CHUNK)))
-            xz[1, c] = quantise_chunk(1, c, x1[:], stim1[:, :, c * CHUNK : (c + 1) * CHUNK])
+        operands = {
+            (0, 0): quantise("xz0_0", first_grouped[0], tag="gain1"),
+            (0, 1): quantise("xz0_1", first_grouped[1], tag="h1_1"),
+        }
 
-        def read_out(c, pair):
-            y_bank = psum.tile([P, 2, CHUNK], F32, name="y_bank")
-            ab_banks = [psum.tile([P, 2, CHUNK], F32, name="ab_bank%d" % b) for b in range(2)]
+        stim_early = load_planes("stim_early", stim, 1, 0, PAIR, tag="cpl_planes0")
+        stim_late = load_planes("stim_late", stim, 1, PAIR, PAIR, tag="cpl_planes1")
+        last_grouped, z_pairs = [], []
+        for c in range(CHUNKS):
+            pairs = held("z_pairs%d" % c, [P, PACK // PAIR, CHUNK], F32)
+            add_by_transposes(c, pairs[:, :1, :].rearrange("p u m -> p m u"), x_early[:, :, chunk_cols(c)], stim_early[:, :, chunk_cols(c)])
+            grouped = held("grouped1_%d" % c, [P, 2 * CHUNK * PACK], BF16, tag="h0_%d" % c)
+            interleave(grouped[:, x_part], 0, x_early[:, :, chunk_cols(c)])
+            last_grouped.append(grouped)
+            z_pairs.append(pairs)
+
+        late_tags = ("x_early", "cpl_planes0", "h0_0", "h0_1")
+
+        def finish_chunk(c):
+            if (0, c) not in operands:
+                operands[0, c] = quantise("xz0_%d" % c, first_grouped[c], tag="z_pairs%d" % (c - 1))
+            x_late = held("x_late%d" % c, [P, PAIR, CHUNK], F32, tag=late_tags[c])
+            for e in range(PAIR):
+                fetch(x_late[:, e, :], 1, PAIR + e, c * CHUNK, CHUNK)
+            nc.vector.tensor_tensor(
+                z_pairs[c][:, 1, :].bitcast(BF16).rearrange("p (c i e) -> p c e i", i=PACK, e=PAIR),
+                x_late[:].rearrange("p e (c i) -> p c e i", i=PACK),
+                stim_late[:, :, chunk_cols(c)].rearrange("p e (c i) -> p c e i", i=PACK),
+                ADD,
+            )
+            interleave(last_grouped[c][:, x_part], PAIR, x_late[:])
+            nc.scalar.copy(out=column_words(last_grouped[c][:, z_part]), in_=z_pairs[c][:].rearrange("p u m -> p m u"))
+            operands[1, c] = quantise("xz1_%d" % c, last_grouped[c])
+
+        def read_out(c, half):
+            step = 2 * c + half
+            row_tiles = [slice((2 * half + b) * P, (2 * half + b + 1) * P) for b in range(2)]
+            readout = bank(READOUT_BANKS, step, [P, 2, CHUNK])
+            couplings = [bank(COUPLING_BANKS, 2 * step + b, [P, 2, CHUNK]) for b in range(2)]
             for a in range(PASSES):
-                codes, scales = xz[a, c]
-                for b in range(2):
-                    cols = slice((2 * pair + b) * P, (2 * pair + b + 1) * P)
+                codes, scales = operands[a, c]
+                cpl_codes, cpl_scales = coupling[a]
+                for b, rows in enumerate(row_tiles):
                     nc.tensor.matmul_mx(
-                        out=ab_banks[b][:].rearrange("p s m -> p (s m)"),
-                        lhsT=cpl_w[a][:, cols].bitcast(FP8X4), lhsT_scale=cpl_s[a][:, cols],
+                        out=couplings[b][:].rearrange("p s m -> p (s m)"),
+                        lhsT=cpl_codes[:, rows].bitcast(FP8X4), lhsT_scale=cpl_scales[:, rows],
                         rhs=codes[:].bitcast(FP8X4), rhs_scale=scales[:],
                         start=(a == 0), stop=(a == PASSES - 1),
                     )
-                for b in range(2):
-                    cols = slice((2 * pair + b) * P, (2 * pair + b + 1) * P)
+                for b, rows in enumerate(row_tiles):
                     nc.tensor.matmul_mx(
-                        out=y_bank[:, b, :],
-                        lhsT=ro_w[:, a, cols].bitcast(FP8X4), lhsT_scale=ro_s[4 * a :, cols],
+                        out=readout[:, b, :],
+                        lhsT=ro_w[:, a, rows].bitcast(FP8X4), lhsT_scale=ro_s[PACK * a :, rows],
                         rhs=codes[:, CHUNK:].bitcast(FP8X4), rhs_scale=scales[:, CHUNK:],
                         start=(a == 0 and b == 0), stop=(a == PASSES - 1 and b == 1),
                     )
             bent = ring.tile([P, 2, 2, CHUNK], F32, name="bent")
             for b in range(2):
-                nc.scalar.activation(bent[:, b, :, :], ab_banks[b][:], TANH)
+                nc.scalar.activation(bent[:, b, :, :], couplings[b][:], TANH)
             partial = ring.tile([P, 2, CHUNK], F32, name="partial")
-            nc.vector.tensor_tensor(partial[:], y_bank[:], bent[:, :, 0, :], ADD)
+            nc.vector.tensor_tensor(partial[:], readout[:], bent[:, :, 0, :], ADD)
             result = ring.tile([P, 2, CHUNK], F32, name="result")
             nc.vector.tensor_tensor(result[:], partial[:], bent[:, :, 1, :], ADD)
-            rows = out[2 * pair * P : (2 * pair + 2) * P, c * CHUNK : (c + 1) * CHUNK]
-            nc.sync.dma_start(out=rows.rearrange("(b p) m -> p b m", p=P), in_=result[:])
+            rows_out = out[2 * half * P : (2 * half + 2) * P, chunk_cols(c)]
+            nc.sync.dma_start(out=rows_out.rearrange("(b p) m -> p b m", p=P), in_=result[:])
 
-        fetch_chunk(0)
+        finish_chunk(0)
         for c in range(CHUNKS):
             if c + 1 < CHUNKS:
-                fetch_chunk(c + 1)
-            for pair in range(2):
-                read_out(c, pair)
+                finish_chunk(c + 1)
+            for half in range(2):
+                read_out(c, half)

from contextlib import ExitStack

import concourse.mybir as mybir
from concourse.masks import make_identity

K, H, N, T, S, T2, M = 512, 1024, 512, 2048, 1024, 2048, 1024
FLOPS = 2 * K * H * S + 3 * 2 * H * N * M

F32 = mybir.dt.float32
BF16 = mybir.dt.bfloat16
I32 = mybir.dt.int32
U32 = mybir.dt.uint32
U16 = mybir.dt.uint16
U8 = mybir.dt.uint8
FP8X4 = mybir.dt.float8_e4m3fn_x4
FP4X4 = mybir.dt.float4_e2m1fn_x4
MULT = mybir.AluOpType.mult
ADD = mybir.AluOpType.add
TANH = mybir.ActivationFunctionType.Tanh

P = 128
QUADRANT = 32
PACK = 4
K_PASS = P * PACK
PASSES = H // K_PASS
BANK = 512
CHUNK = 256
CHUNKS = M // CHUNK
BLOCKS = CHUNK // P
LIST_ROWS = 16
PAIR = 2
PAGE_BUFS = 4
RING_BUFS = 3
GROUPED_BUFS = CHUNKS

COUPLING_BANKS = (0, 1, 2, 3, 4)
READOUT_BANKS = (5, 6, 7)
H_BANKS = (0, 1, 2)
TURN_BANKS = (3, 4)
BACK_BANK = 7


def tile_list_parcel_coupling_readout_kernel(
    tc, tab_words, tab_scales, offs, w4_words, w4_scales, page0, wgs, offs2, offs3,
    stim, cpl, ro8_words, ro8_scales, out,
):
    nc = tc.nc
    with ExitStack() as ctx:
        keep = ctx.enter_context(tc.tile_pool(name="keep", bufs=1))
        pages = ctx.enter_context(tc.tile_pool(name="pages", bufs=PAGE_BUFS))
        ring = ctx.enter_context(tc.tile_pool(name="ring", bufs=RING_BUFS))
        psum = ctx.enter_context(tc.psum_pool(name="psum", bufs=1))

        def held(name, shape, dtype, tag=None):
            return keep.tile(shape, dtype, align_bytes=64, name=name, tag=tag or name)

        def bank(banks, turn, shape):
            return psum.tile(shape, F32, name="bank%d" % banks[turn % len(banks)])

        def load_list(name, source):
            tile = held(name, list(source.shape), U16)
            nc.sync.dma_start(tile[:], source)
            return tile

        def entries(tile, first, count):
            return tile[:, first // LIST_ROWS : (first + count) // LIST_ROWS]

        def load_scales(tile, source):
            rows = PACK * source.shape[0]
            for q in range(P // QUADRANT):
                nc.sync.dma_start(
                    out=tile[QUADRANT * q : QUADRANT * q + rows, :].bitcast(I32),
                    in_=source[:, PACK * q : PACK * (q + 1), :].bitcast(I32),
                )

        def pass_rows(source, a):
            return source[a * K_PASS : (a + 1) * K_PASS, :].rearrange("(p t) c -> p t c", t=PACK)

        def load_planes(name, source, a, first=0, count=PACK, tag=None):
            tile = held(name, [P, count, source.shape[1]], F32, tag)
            nc.sync.dma_start(out=tile[:], in_=pass_rows(source, a)[:, first : first + count, :])
            return tile

        def load_page(a, t):
            page = pages.tile([P, T2], F32, name="page")
            nc.sync.dma_start(out=page[:], in_=pass_rows(page0, a)[:, t, :])
            return page

        def load_gain(t):
            gain = held("gain%d" % t, [P, S], F32)
            rows = wgs.rearrange("(q t) j -> q t j", t=PACK)[:, t, :]
            for q in range(P // QUADRANT):
                nc.sync.dma_start(out=gain[QUADRANT * q : QUADRANT * (q + 1), :], in_=rows)
            return gain

        def chunk_cols(c):
            return slice(c * CHUNK, (c + 1) * CHUNK)

        def interleave(grouped, first, planes):
            places = grouped.rearrange("p (c i t) -> p c t i", i=PACK, t=PACK)
            nc.scalar.copy(
                out=places[:, :, first : first + planes.shape[1], :],
                in_=planes.rearrange("p t (c i) -> p c t i", i=PACK),
            )

        def quantise(name, grouped, tag=None):
            width = grouped.shape[1] // PACK
            codes = held(name + "_codes", [P, width], U32, tag)
            scales = held(name + "_scales", [P, width], U8)
            nc.vector.quantize_mx(out=codes[:].bitcast(FP8X4), scales=scales[:], in_=grouped[:])
            return codes, scales

        tab_s = held("tab_s", [P, T], U8)
        w4_s_raw = held("w4_s_raw", [P, H], U8)
        nc.gpsimd.memset(tab_s[:].bitcast(I32), 0)
        nc.vector.memset(w4_s_raw[:].bitcast(I32), 0)
        w4_w_raw = held("w4_w_raw", [P, H], U16)
        nc.sync.dma_start(out=w4_w_raw[:].bitcast(I32), in_=w4_words[0].bitcast(I32))
        idx = load_list("idx", offs)
        load_scales(tab_s, tab_scales)
        tab_w = held("tab_w", [P, T], U32)
        nc.sync.dma_start(out=tab_w[:].bitcast(I32), in_=tab_words[0].rearrange("p t i -> p (t i)").bitcast(I32))
        load_scales(w4_s_raw, w4_scales)
        ident = held("ident", [P, P], F32)
        make_identity(nc, ident[:])
        page_tiles = {(0, 0): load_page(0, 0)}
        idx2 = load_list("idx2", offs2)
        gains = [load_gain(0)]
        page_tiles[0, 1] = load_page(0, 1)
        idx3 = load_list("idx3", offs3)
        gains.append(load_gain(1))

        def columns_by_plane(name, raw):
            tile = held(name, [P, H], raw.dtype)
            nc.vector.tensor_copy(
                out=tile[:].rearrange("p (a t m) -> p a t m", a=PASSES, t=PACK),
                in_=raw[:].rearrange("p (a m t) -> p a t m", a=PASSES, t=PACK),
            )
            return tile

        def gather_table(name, table, half, tag=None):
            tile = held("%s%d" % (name, half), [P, BANK], table.dtype, tag)
            nc.vector.tensor_copy(tile[:], table[:].indirect(entries(idx, half * BANK, BANK)))
            return tile

        w4_w = columns_by_plane("w4_w", w4_w_raw)
        v_s = [gather_table("v_s", tab_s, 0)]
        v_w = [gather_table("v_w", tab_w, 0)]
        w4_s = columns_by_plane("w4_s", w4_s_raw)
        v_s.append(gather_table("v_s", tab_s, 1))
        v_w.append(gather_table("v_w", tab_w, 1, tag="w4_s_raw"))

        def reset_plane(a, t):
            plane = a * PACK + t
            cols = slice(plane * P, (plane + 1) * P)
            h = held("h%d_%d" % (a, t), [P, S], F32)
            for half in range(S // BANK):
                h_bank = bank(H_BANKS, plane * (S // BANK) + half, [P, BANK])
                nc.tensor.matmul_mx(
                    out=h_bank[:],
                    lhsT=w4_w[:, cols].bitcast(U8).bitcast(FP4X4), lhsT_scale=w4_s[:, cols],
                    rhs=v_w[half][:].bitcast(FP8X4), rhs_scale=v_s[half][:],
                    start=True, stop=True,
                )
                nc.scalar.copy(out=h[:, half * BANK : (half + 1) * BANK], in_=h_bank[:])
            width = BANK if plane == 0 else S
            for first in range(0, S, width):
                js = slice(first, first + width)
                window = page_tiles[a, t][:].indirect(entries(idx2, first, width))
                nc.vector.tensor_tensor(window, h[:, js], gains[t][:, js], MULT)

        def fetch(dst, a, t, first, count):
            nc.vector.tensor_copy(dst, page_tiles[a, t][:].indirect(entries(idx3, first, count)))

        def add_by_transposes(c, z_words, x_planes, stim_planes):
            words = x_planes.shape[1] // PAIR
            pieces = [(b, u) for b in range(BLOCKS) for u in range(words)]
            per_bank = BANK // (PAIR * P)
            back = bank((BACK_BANK,), 0, [P, BLOCKS, words, P])
            for turn in range(len(pieces) // per_bank):
                mine = pieces[turn * per_bank : (turn + 1) * per_bank]
                sums = bank(TURN_BANKS, c + turn, [P, per_bank, PAIR, P])
                terms = [(planes, i, e) for planes in (stim_planes, x_planes) for i in range(per_bank) for e in range(PAIR)]
                for number, (planes, i, e) in enumerate(terms):
                    b, u = mine[i]
                    nc.tensor.matmul(
                        sums[:, i, e, :], planes[:, PAIR * u + e, b * P : (b + 1) * P], ident[:], is_transpose=True,
                        start=(number == 0), stop=(number == len(terms) - 1),
                    )
                turned = ring.tile([P, per_bank, P, PAIR], BF16, name="turned")
                nc.scalar.copy(out=turned[:], in_=sums[:].rearrange("m i e p -> m i p e"))
                turned_words = turned[:].rearrange("m i p e -> m i (p e)").bitcast(F32)
                for i, (b, u) in enumerate(mine):
                    nc.tensor.transpose(back[:, b, u, :], turned_words[:, i, :], ident[:])
            nc.scalar.copy(out=z_words.rearrange("p (b m) u -> p b m u", b=BLOCKS), in_=back[:].rearrange("p b u m -> p b m u"))

        def column_words(grouped):
            return grouped.bitcast(F32).rearrange("p (m u) -> p m u", u=PACK // PAIR)

        x_part, z_part = slice(0, CHUNK * PACK), slice(CHUNK * PACK, 2 * CHUNK * PACK)

        coupling = []
        for a in range(PASSES):
            cpl_planes = load_planes("cpl_planes%d" % a, cpl, a)
            grouped = ring.tile([P, N * PACK], BF16, align_bytes=64, name="grouped", bufs=GROUPED_BUFS)
            interleave(grouped[:], 0, cpl_planes[:])
            coupling.append(quantise("cpl%d" % a, grouped))

        x_first = held("x_first", [P, PACK, M], F32)
        for t in range(PACK):
            if t + 2 < PACK:
                page_tiles[0, t + 2] = load_page(0, t + 2)
                gains.append(load_gain(t + 2))
            reset_plane(0, t)
            fetch(x_first[:, t, :], 0, t, 0, M)
        stim_first = load_planes("stim_first", stim, 0)

        ro_w = held("ro_w", [P, PASSES, N], U32)
        nc.sync.dma_start(out=ro_w[:].bitcast(I32), in_=ro8_words.rearrange("a p c i -> p a (c i)").bitcast(I32))
        ro_s = held("ro_s", [P, N], U8)
        nc.vector.memset(ro_s[:].bitcast(I32), 0)
        load_scales(ro_s, ro8_scales)

        x_early = held("x_early", [P, PAIR, M], F32)
        first_grouped = []
        for t in range(PACK):
            page_tiles[1, t] = load_page(1, t)
            reset_plane(1, t)
            if t < PAIR:
                fetch(x_early[:, t, :], 1, t, 0, M)
            grouped = ring.tile([P, 2 * CHUNK * PACK], BF16, align_bytes=64, name="grouped", bufs=GROUPED_BUFS)
            add_by_transposes(t, column_words(grouped[:, z_part]), x_first[:, :, chunk_cols(t)], stim_first[:, :, chunk_cols(t)])
            interleave(grouped[:, x_part], 0, x_first[:, :, chunk_cols(t)])
            first_grouped.append(grouped)

        operands = {
            (0, 0): quantise("xz0_0", first_grouped[0], tag="gain1"),
            (0, 1): quantise("xz0_1", first_grouped[1], tag="h1_1"),
        }

        stim_early = load_planes("stim_early", stim, 1, 0, PAIR, tag="cpl_planes0")
        stim_late = load_planes("stim_late", stim, 1, PAIR, PAIR, tag="cpl_planes1")
        last_grouped, z_pairs = [], []
        for c in range(CHUNKS):
            pairs = held("z_pairs%d" % c, [P, PACK // PAIR, CHUNK], F32)
            add_by_transposes(c, pairs[:, :1, :].rearrange("p u m -> p m u"), x_early[:, :, chunk_cols(c)], stim_early[:, :, chunk_cols(c)])
            grouped = held("grouped1_%d" % c, [P, 2 * CHUNK * PACK], BF16, tag="h0_%d" % c)
            interleave(grouped[:, x_part], 0, x_early[:, :, chunk_cols(c)])
            last_grouped.append(grouped)
            z_pairs.append(pairs)

        late_tags = ("x_early", "cpl_planes0", "h0_0", "h0_1")

        def finish_chunk(c):
            if (0, c) not in operands:
                operands[0, c] = quantise("xz0_%d" % c, first_grouped[c], tag="z_pairs%d" % (c - 1))
            x_late = held("x_late%d" % c, [P, PAIR, CHUNK], F32, tag=late_tags[c])
            for e in range(PAIR):
                fetch(x_late[:, e, :], 1, PAIR + e, c * CHUNK, CHUNK)
            nc.vector.tensor_tensor(
                z_pairs[c][:, 1, :].bitcast(BF16).rearrange("p (c i e) -> p c e i", i=PACK, e=PAIR),
                x_late[:].rearrange("p e (c i) -> p c e i", i=PACK),
                stim_late[:, :, chunk_cols(c)].rearrange("p e (c i) -> p c e i", i=PACK),
                ADD,
            )
            interleave(last_grouped[c][:, x_part], PAIR, x_late[:])
            nc.scalar.copy(out=column_words(last_grouped[c][:, z_part]), in_=z_pairs[c][:].rearrange("p u m -> p m u"))
            operands[1, c] = quantise("xz1_%d" % c, last_grouped[c])

        def read_out(c, half):
            step = 2 * c + half
            row_tiles = [slice((2 * half + b) * P, (2 * half + b + 1) * P) for b in range(2)]
            readout = bank(READOUT_BANKS, step, [P, 2, CHUNK])
            couplings = [bank(COUPLING_BANKS, 2 * step + b, [P, 2, CHUNK]) for b in range(2)]
            for a in range(PASSES):
                codes, scales = operands[a, c]
                cpl_codes, cpl_scales = coupling[a]
                for b, rows in enumerate(row_tiles):
                    nc.tensor.matmul_mx(
                        out=couplings[b][:].rearrange("p s m -> p (s m)"),
                        lhsT=cpl_codes[:, rows].bitcast(FP8X4), lhsT_scale=cpl_scales[:, rows],
                        rhs=codes[:].bitcast(FP8X4), rhs_scale=scales[:],
                        start=(a == 0), stop=(a == PASSES - 1),
                    )
                for b, rows in enumerate(row_tiles):
                    nc.tensor.matmul_mx(
                        out=readout[:, b, :],
                        lhsT=ro_w[:, a, rows].bitcast(FP8X4), lhsT_scale=ro_s[PACK * a :, rows],
                        rhs=codes[:, CHUNK:].bitcast(FP8X4), rhs_scale=scales[:, CHUNK:],
                        start=(a == 0 and b == 0), stop=(a == PASSES - 1 and b == 1),
                    )
            bent = ring.tile([P, 2, 2, CHUNK], F32, name="bent")
            for b in range(2):
                nc.scalar.activation(bent[:, b, :, :], couplings[b][:], TANH)
            partial = ring.tile([P, 2, CHUNK], F32, name="partial")
            nc.vector.tensor_tensor(partial[:], readout[:], bent[:, :, 0, :], ADD)
            result = ring.tile([P, 2, CHUNK], F32, name="result")
            nc.vector.tensor_tensor(result[:], partial[:], bent[:, :, 1, :], ADD)
            rows_out = out[2 * half * P : (2 * half + 2) * P, chunk_cols(c)]
            nc.sync.dma_start(out=rows_out.rearrange("(b p) m -> p b m", p=P), in_=result[:])

        finish_chunk(0)
        for c in range(CHUNKS):
            if c + 1 < CHUNKS:
                finish_chunk(c + 1)
            for half in range(2):
                read_out(c, half)
